import numpy as np
import ml_dtypes


def mxq(x, axis, fmt="e4m3"):
    dtype, down = {"e4m3": (ml_dtypes.float8_e4m3fn, 7), "e5m2": (ml_dtypes.float8_e5m2, 14)}[fmt]
    v = np.moveaxis(np.asarray(x, np.float32).astype(ml_dtypes.bfloat16).astype(np.float64), axis, -1)
    blocks = v.reshape(v.shape[:-1] + (-1, 32))
    amax = np.abs(blocks).max(-1, keepdims=True)
    byte = np.maximum(np.where(amax > 0, np.frexp(amax)[1] - 1 + 127, 0) - down, 1)
    scale = np.exp2(byte - 127.0)
    codes = (blocks / scale).astype(np.float32).astype(dtype).astype(np.float64)
    return np.moveaxis((codes * scale).reshape(v.shape), -1, axis)


WIDE = False


def mx_kscale(k):
    if not WIDE:
        return np.ones(k)
    levels = np.array([10, -10, 5, -5, 0])
    if k % 512:
        return np.exp2(np.random.permutation(np.resize(levels, k // 32))).repeat(32)
    a = np.empty((k // 512, 16))
    for p in range(k // 512):
        a[p, :8] = np.random.permutation(np.resize(levels, 8))
        for g in range(8):
            far = levels[np.abs(levels - a[p, g]) >= 10]
            a[p, g + 8] = far[np.random.randint(len(far))]
    return np.exp2(a.ravel()).repeat(32)


def f64(x):
    return np.asarray(x).astype(np.float64)


def striped(idx):
    return np.tile(idx.reshape(-1, 16).T, (8, 1)).astype(np.uint16)


def unstriped(offs):
    return offs[:16].T.reshape(-1).astype(np.int64)


E2M1 = np.array([0.0, 0.5, 1.0, 1.5, 2.0, 3.0, 4.0, 6.0, -0.0, -0.5, -1.0, -1.5, -2.0, -3.0, -4.0, -6.0])


def pack_weight(w, fmt):
    k, n = w.shape
    w = f64(np.asarray(w, np.float32).astype(ml_dtypes.bfloat16)).reshape(k // 32, 32, n)
    amax = np.abs(w).max(1)
    if fmt == "e4m3":
        byte = np.frexp(amax)[1] - 1 + 127 - 7
    else:
        mant, ex = np.frexp(amax / 6.0)
        byte = np.where(mant > 0.5, ex, ex - 1) + 127
    byte = np.clip(np.where(amax > 0, byte, 1), 1, 254)
    scaled = (w * np.exp2(127.0 - byte)[:, None, :]).reshape(k, n).astype(np.float32)
    by_word = np.ascontiguousarray(scaled.reshape(k // 512, 128, 4, n).transpose(0, 1, 3, 2))
    if fmt == "e4m3":
        words = by_word.astype(ml_dtypes.float8_e4m3fn).view(np.uint8)
    else:
        c = by_word.astype(ml_dtypes.float4_e2m1fn).view(np.uint8) & 0xF
        words = (c[..., 0::2] | (c[..., 1::2] << 4)).reshape(k // 512, 128, 2 * n)
    return np.ascontiguousarray(words), np.ascontiguousarray(byte.astype(np.uint8).reshape(k // 512, 16, n))


def unpack_weight(words, scales, fmt):
    g, _, n = scales.shape
    words = np.ascontiguousarray(words).reshape(g, 128, n, -1)
    if fmt == "e4m3":
        vals = words.view(ml_dtypes.float8_e4m3fn).astype(np.float64)
    else:
        nib = np.empty((g, 128, n, 4), np.uint8)
        nib[..., 0::2] = words & 0xF
        nib[..., 1::2] = words >> 4
        vals = E2M1[nib]
    vals = vals * np.repeat(np.exp2(scales.astype(np.float64) - 127.0), 8, axis=1)[..., None]
    return vals.transpose(0, 1, 3, 2).reshape(g * 512, n)


def gelu(v):
    return 0.5 * v * (1.0 + np.tanh(np.sqrt(2.0 / np.pi) * (v + 0.044715 * v**3)))


K, H, T, S, T2, P = 512, 1024, 4096, 1024, 2048, 512

def setup_inputs():
    n = np.random.standard_normal
    s = mx_kscale(K)[:, None]
    u = mx_kscale(H)[:, None]
    tab_words, tab_scales = pack_weight(n((K, T)) * s, "e4m3")
    w1 = n((K, H)) / np.sqrt(K) / s * u.T
    w2_words, w2_scales = pack_weight(n((K, H)) / np.sqrt(K) / s * u.T, "e2m1")
    w3_words, w3_scales = pack_weight(n((K, H)) / np.sqrt(K) / s * u.T, "e4m3")
    w4 = n((H, H)) / np.sqrt(H) / u * u.T
    return {
        "tab_words": tab_words, "tab_scales": tab_scales,
        "offs": striped(np.random.permutation(T)[:S]),
        "w1": w1.astype(np.float32),
        "w2_words": w2_words, "w2_scales": w2_scales,
        "w3_words": w3_words, "w3_scales": w3_scales,
        "page0": (n((H, T2)) * u).astype(np.float32),
        "offs2": striped(np.random.permutation(T2)[:S]),
        "offs3": striped(np.random.permutation(T2)[:P]),
        "aspect": np.exp(0.5 * n((H, P))).astype(np.float32),
        "w4": w4.astype(np.float32),
    }

def reference(tab_words, tab_scales, offs, w1, w2_words, w2_scales, w3_words, w3_scales,
              page0, offs2, offs3, aspect, w4):
    v = unpack_weight(tab_words, tab_scales, "e4m3")[:, unstriped(offs)]
    h1 = mxq(f64(w1), 0, "e4m3").T @ v
    h2 = unpack_weight(w2_words, w2_scales, "e2m1").T @ v
    h3 = unpack_weight(w3_words, w3_scales, "e4m3").T @ v
    h = np.maximum(np.maximum(h1, h2), h3)
    page = f64(page0).copy()
    l2 = unstriped(offs2)
    page[:, l2] = page[:, l2] + h
    x = page[:, unstriped(offs3)] * f64(aspect)
    y = mxq(f64(w4), 0, "e4m3").T @ mxq(x, 0, "e4m3")
    return np.maximum(y, x)

@@ -1,0 +1,233 @@
+from contextlib import ExitStack
+
+import concourse.mybir as mybir
+
+K, H, T, S, T2, NJ = 512, 1024, 4096, 1024, 2048, 512
+FLOPS = 2 * K * H * S * 3 + 2 * H * H * NJ
+
+F32 = mybir.dt.float32
+BF16 = mybir.dt.bfloat16
+I32 = mybir.dt.int32
+U32 = mybir.dt.uint32
+U16 = mybir.dt.uint16
+U8 = mybir.dt.uint8
+FP8X4 = mybir.dt.float8_e4m3fn_x4
+FP4X4 = mybir.dt.float4_e2m1fn_x4
+ALU = mybir.AluOpType
+
+P = 128
+PACK = 4
+KP = P * PACK
+BANK = 512
+BLOCKS = H // KP
+SLICES = H // P
+JH = NJ // 2
+
+
+def tile_list_slope_loading_page_kernel(
+    tc, tab_words, tab_scales, offs, w1, w2_words, w2_scales, w3_words, w3_scales,
+    page0, offs2, offs3, aspect, w4, out,
+):
+    nc = tc.nc
+    page_rows = page0.rearrange("(b p t) c -> b t p c", p=P, t=PACK)
+    aspect_rows = aspect.rearrange("(b p t) c -> b t p c", p=P, t=PACK)
+    out_rows = out.rearrange("(b p t) c -> b p t c", p=P, t=PACK)
+    w1_rows = w1.rearrange("(p i) c -> p i c", i=PACK)
+    w4_rows = w4.rearrange("(b p i) c -> b p i c", p=P, i=PACK)
+
+    with ExitStack() as ctx:
+        keep = ctx.enter_context(tc.tile_pool(name="keep", bufs=1))
+        ring = ctx.enter_context(tc.tile_pool(name="ring", bufs=2))
+        pages = ctx.enter_context(tc.tile_pool(name="pages", bufs=4))
+        psum = ctx.enter_context(tc.psum_pool(name="psum", bufs=1))
+
+        idx = keep.tile([P, S // 16], U16, name="idx")
+        idx2 = keep.tile([P, S // 16], U16, name="idx2")
+        idx3 = keep.tile([P, NJ // 16], U16, name="idx3")
+        tab_w = keep.tile([P, T], U32, name="tab_w")
+        tab_s = keep.tile([P, T], U8, name="tab_s")
+        v_w = keep.tile([P, S], U32, name="v_w", align_bytes=64)
+        v_s = keep.tile([P, S], U8, name="v_s", align_bytes=64)
+        w2_raw = keep.tile([P, 2 * H], U8, name="w2_raw")
+        w3_raw = keep.tile([P, H], I32, name="w3_raw")
+        ws_raw = keep.tile([P, H], U8, name="ws_raw")
+        w2_c = keep.tile([P, 2 * H], U8, name="w2_c", align_bytes=64)
+        w3_c = keep.tile([P, H], I32, name="w3_c", align_bytes=64)
+        w23_s = keep.tile([P, H], U8, name="w23_s", align_bytes=64)
+        w1_c = [keep.tile([P, KP], U32, name="w1_c%d" % b, align_bytes=64) for b in range(BLOCKS)]
+        w1_s = [keep.tile([P, KP], U8, name="w1_s%d" % b, align_bytes=64) for b in range(BLOCKS)]
+        w4_c = [keep.tile([P, KP], U32, name="w4_c%d" % q, align_bytes=64) for q in range(BLOCKS * BLOCKS)]
+        w4_s = [keep.tile([P, KP], U8, name="w4_s%d" % q, align_bytes=64) for q in range(BLOCKS * BLOCKS)]
+        x = [keep.tile([P, PACK, NJ], F32, name="x%d" % b) for b in range(BLOCKS)]
+        x_c = [[keep.tile([P, JH], U32, name="x_c%d%d" % (b, u), align_bytes=64) for u in range(2)] for b in range(BLOCKS)]
+        x_s = [[keep.tile([P, JH], U8, name="x_s%d%d" % (b, u), align_bytes=64) for u in range(2)] for b in range(BLOCKS)]
+        asp = [keep.tile([P, NJ], F32, name="asp%d" % s) for s in range(SLICES)]
+
+        def load_scale_rows(queue, plane, rows, first):
+            for q in range(4):
+                queue.dma_start(
+                    out=plane[32 * q + first : 32 * q + first + 4, :].bitcast(I32),
+                    in_=rows[0, 4 * q : 4 * q + 4, :].bitcast(I32),
+                )
+
+        def load_page(s):
+            page = pages.tile([P, T2], F32, name="page")
+            nc.sync.dma_start(out=page[:], in_=page_rows[s // PACK, s % PACK])
+            return page
+
+        def load_weight(rows):
+            raw = ring.tile([P, PACK, KP], F32, name="w_raw", bufs=3)
+            nc.sync.dma_start(out=raw[:], in_=rows)
+            return raw
+
+        def round_weight(raw):
+            rounded = ring.tile([P, PACK * KP], BF16, name="w_bf", align_bytes=64)
+            nc.scalar.copy(
+                out=rounded[:].rearrange("p (t m i) -> p m t i", t=PACK, i=PACK),
+                in_=raw[:].rearrange("p i (m t) -> p m t i", t=PACK),
+            )
+            return rounded[:]
+
+        def quantize(codes, scales, rounded):
+            nc.vector.quantize_mx(out=codes[:].bitcast(FP8X4), scales=scales[:], in_=rounded)
+
+        def fetch_old(page):
+            old = ring.tile([P, S], F32, name="old")
+            nc.vector.tensor_copy(out=old[:], in_=page[:].indirect(idx2[:]))
+            return old
+
+        def features(s):
+            b, t = divmod(s, PACK)
+            own = slice(t * P, (t + 1) * P)
+            cols = slice(s * P, (s + 1) * P)
+            h1 = ring.tile([P, S], F32, name="h1")
+            h13 = ring.tile([P, S], F32, name="h13")
+            h = ring.tile([P, S], F32, name="h")
+            banks = []
+            for u in range(S // BANK):
+                j = slice(u * BANK, (u + 1) * BANK)
+                rhs = dict(rhs=v_w[:, j].bitcast(FP8X4), rhs_scale=v_s[:, j], start=True, stop=True)
+                acc = [psum.tile([P, BANK], F32, name="bank%d" % (3 * u + i)) for i in range(3)]
+                nc.tensor.matmul_mx(out=acc[0][:], lhsT=w1_c[b][:, own].bitcast(FP8X4), lhsT_scale=w1_s[b][:, own], **rhs)
+                nc.tensor.matmul_mx(out=acc[1][:], lhsT=w3_c[:, cols].bitcast(FP8X4), lhsT_scale=w23_s[4:P, cols], **rhs)
+                nc.tensor.matmul_mx(
+                    out=acc[2][:], lhsT=w2_c[:, 2 * s * P : 2 * (s + 1) * P].bitcast(FP4X4), lhsT_scale=w23_s[:, cols], **rhs
+                )
+                nc.scalar.copy(out=h1[:, j], in_=acc[0][:])
+                banks.append((j, acc))
+            for j, acc in banks:
+                nc.vector.tensor_tensor(out=h13[:, j], in0=acc[1][:], in1=h1[:, j], op=ALU.max)
+            for j, acc in banks:
+                nc.vector.tensor_tensor(out=h[:, j], in0=acc[2][:], in1=h13[:, j], op=ALU.max)
+            return h
+
+        def put_new(page, old, h):
+            nc.vector.tensor_tensor(out=page[:].indirect(idx2[:]), in0=old[:], in1=h[:], op=ALU.add)
+
+        def fetch_x(s, page, parts):
+            b, t = divmod(s, PACK)
+            width = NJ // parts
+            for u in range(parts):
+                j = slice(u * width, (u + 1) * width)
+                listed = idx3[:, u * width // 16 : (u + 1) * width // 16]
+                nc.vector.tensor_tensor(out=x[b][:, t, j], in0=page[:].indirect(listed), in1=asp[s][:, j], op=ALU.mult)
+
+        def round_x(b, u):
+            rounded = ring.tile([P, JH, PACK], BF16, name="x_bf", align_bytes=64)
+            nc.scalar.copy(
+                out=rounded[:].rearrange("p (c e) t -> p c t e", e=4),
+                in_=x[b][:, :, u * JH : (u + 1) * JH].rearrange("p t (c e) -> p c t e", e=4),
+            )
+            return rounded[:].rearrange("p j t -> p (j t)")
+
+        def mix_pass(bank, b, u, nb, pair):
+            for e in range(2):
+                t = 2 * pair + e
+                own = slice(t * P, (t + 1) * P)
+                nc.tensor.matmul_mx(
+                    out=bank[:, e, :],
+                    lhsT=w4_c[BLOCKS * b + nb][:, own].bitcast(FP8X4),
+                    lhsT_scale=w4_s[BLOCKS * b + nb][:, own],
+                    rhs=x_c[b][u][:].bitcast(FP8X4),
+                    rhs_scale=x_s[b][u][:],
+                    start=(b == 0 and e == 0),
+                    stop=(b == BLOCKS - 1 and e == 1),
+                )
+
+        nc.vector.memset(tab_s[:].bitcast(I32), 0)
+        nc.gpsimd.memset(ws_raw[:].bitcast(I32), 0)
+        nc.sync.dma_start(idx2[:], offs2)
+        page = {0: load_page(0)}
+        load_scale_rows(nc.scalar, tab_s, tab_scales, 0)
+        nc.sync.dma_start(idx[:], offs)
+        nc.sync.dma_start(out=tab_w[:].bitcast(I32), in_=tab_words[0].rearrange("p t i -> p (t i)").bitcast(I32))
+        load_scale_rows(nc.scalar, ws_raw, w3_scales, 4)
+        load_scale_rows(nc.scalar, ws_raw, w2_scales, 0)
+        w1_raw = load_weight(w1_rows[:, :, 0:KP])
+        nc.sync.dma_start(out=w3_raw[:], in_=w3_words[0].rearrange("p c i -> p (c i)").bitcast(I32))
+        nc.sync.dma_start(out=w2_raw[:].bitcast(I32), in_=w2_words[0].bitcast(I32))
+        page[1] = load_page(1)
+        nc.sync.dma_start(idx3[:], offs3)
+        nc.sync.dma_start(out=asp[0][:], in_=aspect_rows[0, 0])
+
+        old = fetch_old(page[0])
+        rounded = round_weight(w1_raw)
+        nc.vector.tensor_copy(out=v_s[:], in_=tab_s[:].indirect(idx[:]))
+        nc.vector.tensor_copy(
+            out=w3_c[:].rearrange("p (b t m) -> p b m t", t=PACK, m=P),
+            in_=w3_raw[:].rearrange("p (b m t) -> p b m t", t=PACK, m=P),
+        )
+        nc.vector.tensor_copy(
+            out=w2_c[:].bitcast(U16).rearrange("p (b t m) -> p b t m", t=PACK, m=P),
+            in_=w2_raw[:].bitcast(U16).rearrange("p (b m t) -> p b t m", t=PACK, m=P),
+        )
+        nc.vector.tensor_copy(
+            out=w23_s[:].rearrange("p (b t m) -> p b t m", t=PACK, m=P),
+            in_=ws_raw[:].rearrange("p (b m t) -> p b t m", t=PACK, m=P),
+        )
+        quantize(w1_c[0], w1_s[0], rounded)
+        for u in range(S // BANK):
+            nc.vector.tensor_copy(
+                out=v_w[:, u * BANK : (u + 1) * BANK],
+                in_=tab_w[:].indirect(idx[:, u * BANK // 16 : (u + 1) * BANK // 16]),
+            )
+        h = features(0)
+
+        later_weights = [(w1_rows[:, :, KP:H], w1_c[1], w1_s[1])] + [
+            (w4_rows[b, :, :, nb * KP : (nb + 1) * KP], w4_c[BLOCKS * b + nb], w4_s[BLOCKS * b + nb])
+            for b in range(BLOCKS)
+            for nb in range(BLOCKS)
+        ]
+        for s in range(SLICES):
+            if s + 2 < SLICES:
+                page[s + 2] = load_page(s + 2)
+            if s + 1 < SLICES:
+                nc.sync.dma_start(out=asp[s + 1][:], in_=aspect_rows[(s + 1) // PACK, (s + 1) % PACK])
+            if s < len(later_weights):
+                rows, codes, scales = later_weights[s]
+                rounded = round_weight(load_weight(rows))
+            put_new(page[s], old, h)
+            if s < len(later_weights):
+                quantize(codes, scales, rounded)
+            if s == PACK:
+                for u in range(2):
+                    quantize(x_c[0][u], x_s[0][u], round_x(0, u))
+            if s + 1 < SLICES:
+                old = fetch_old(page[s + 1])
+                h = features(s + 1)
+                fetch_x(s, page[s], 1)
+
+        parts = [(u, nb, pair) for u in range(2) for nb in range(BLOCKS) for pair in range(2)]
+        banks = [psum.tile([P, 2, JH], F32, name="bank%d" % i) for i in range(len(parts))]
+        for bank, part in zip(banks, parts):
+            mix_pass(bank, 0, *part)
+        fetch_x(SLICES - 1, page[SLICES - 1], 2)
+        for u in range(2):
+            quantize(x_c[1][u], x_s[1][u], round_x(1, u))
+        for bank, (u, nb, pair) in zip(banks, parts):
+            mix_pass(bank, 1, u, nb, pair)
+            j = slice(u * JH, (u + 1) * JH)
+            t = slice(2 * pair, 2 * pair + 2)
+            result = ring.tile([P, 2, JH], F32, name="result", bufs=8)
+            nc.vector.tensor_tensor(out=result[:], in0=bank[:], in1=x[nb][:, t, j], op=ALU.max)
+            nc.sync.dma_start(out=out_rows[nb, :, t, j], in_=result[:])

@@ -21,7 +21,7 @@ KP = P * PACK
 BANK = 512
 BLOCKS = H // KP
 SLICES = H // P
-JH = NJ // 2
+PIECES = (slice(0, NJ // 2), slice(NJ // 2, NJ))
 
 
 def tile_list_slope_loading_page_kernel(
@@ -54,18 +54,12 @@ def tile_list_slope_loading_page_kernel(
         w2_c = keep.tile([P, 2 * H], U8, name="w2_c", align_bytes=64)
         w3_c = keep.tile([P, H], I32, name="w3_c", align_bytes=64)
         w23_s = keep.tile([P, H], U8, name="w23_s", align_bytes=64)
-        w1_c = [keep.tile([P, KP], U32, name="w1_c%d" % b, align_bytes=64) for b in range(BLOCKS)]
-        w1_s = [keep.tile([P, KP], U8, name="w1_s%d" % b, align_bytes=64) for b in range(BLOCKS)]
-        w4_c = [keep.tile([P, KP], U32, name="w4_c%d" % q, align_bytes=64) for q in range(BLOCKS * BLOCKS)]
-        w4_s = [keep.tile([P, KP], U8, name="w4_s%d" % q, align_bytes=64) for q in range(BLOCKS * BLOCKS)]
-        x = [keep.tile([P, PACK, NJ], F32, name="x%d" % b) for b in range(BLOCKS)]
-        x_c = [[keep.tile([P, JH], U32, name="x_c%d%d" % (b, u), align_bytes=64) for u in range(2)] for b in range(BLOCKS)]
-        x_s = [[keep.tile([P, JH], U8, name="x_s%d%d" % (b, u), align_bytes=64) for u in range(2)] for b in range(BLOCKS)]
-        asp = [keep.tile([P, NJ], F32, name="asp%d" % s) for s in range(SLICES)]
+        x = [keep.tile([P, PACK - b, NJ], F32, name="x%d" % b) for b in range(BLOCKS)]
+        x_last = [keep.tile([P, j.stop - j.start], F32, name="x_last%d" % u) for u, j in enumerate(PIECES)]
 
-        def load_scale_rows(queue, plane, rows, first):
+        def load_scale_rows(plane, rows, first):
             for q in range(4):
-                queue.dma_start(
+                nc.scalar.dma_start(
                     out=plane[32 * q + first : 32 * q + first + 4, :].bitcast(I32),
                     in_=rows[0, 4 * q : 4 * q + 4, :].bitcast(I32),
                 )
@@ -74,6 +68,11 @@ def tile_list_slope_loading_page_kernel(
             page = pages.tile([P, T2], F32, name="page")
             nc.sync.dma_start(out=page[:], in_=page_rows[s // PACK, s % PACK])
             return page
+
+        def load_aspect(s):
+            rows = keep.tile([P, NJ], F32, name="aspect%d" % s, align_bytes=64)
+            nc.sync.dma_start(out=rows[:], in_=aspect_rows[s // PACK, s % PACK])
+            return rows
 
         def load_weight(rows):
             raw = ring.tile([P, PACK, KP], F32, name="w_raw", bufs=3)
@@ -88,18 +87,23 @@ def tile_list_slope_loading_page_kernel(
             )
             return rounded[:]
 
-        def quantize(codes, scales, rounded):
+        def quantize(rounded, tag):
+            width = rounded.shape[1] // PACK
+            codes = keep.tile([P, width], U32, name="codes", tag=tag, align_bytes=64)
+            scales = keep.tile([P, width], U8, name="scales", tag=tag + "_scales", align_bytes=64)
             nc.vector.quantize_mx(out=codes[:].bitcast(FP8X4), scales=scales[:], in_=rounded)
+            return codes, scales
 
-        def fetch_old(page):
+        def fetch_old(s):
             old = ring.tile([P, S], F32, name="old")
-            nc.vector.tensor_copy(out=old[:], in_=page[:].indirect(idx2[:]))
+            nc.vector.tensor_copy(out=old[:], in_=page[s][:].indirect(idx2[:]))
             return old
 
         def features(s):
             b, t = divmod(s, PACK)
             own = slice(t * P, (t + 1) * P)
             cols = slice(s * P, (s + 1) * P)
+            w1_c, w1_s = w1_mx[b]
             h1 = ring.tile([P, S], F32, name="h1")
             h13 = ring.tile([P, S], F32, name="h13")
             h = ring.tile([P, S], F32, name="h")
@@ -108,7 +112,7 @@ def tile_list_slope_loading_page_kernel(
                 j = slice(u * BANK, (u + 1) * BANK)
                 rhs = dict(rhs=v_w[:, j].bitcast(FP8X4), rhs_scale=v_s[:, j], start=True, stop=True)
                 acc = [psum.tile([P, BANK], F32, name="bank%d" % (3 * u + i)) for i in range(3)]
-                nc.tensor.matmul_mx(out=acc[0][:], lhsT=w1_c[b][:, own].bitcast(FP8X4), lhsT_scale=w1_s[b][:, own], **rhs)
+                nc.tensor.matmul_mx(out=acc[0][:], lhsT=w1_c[:, own].bitcast(FP8X4), lhsT_scale=w1_s[:, own], **rhs)
                 nc.tensor.matmul_mx(out=acc[1][:], lhsT=w3_c[:, cols].bitcast(FP8X4), lhsT_scale=w23_s[4:P, cols], **rhs)
                 nc.tensor.matmul_mx(
                     out=acc[2][:], lhsT=w2_c[:, 2 * s * P : 2 * (s + 1) * P].bitcast(FP4X4), lhsT_scale=w23_s[:, cols], **rhs
@@ -121,57 +125,61 @@ def tile_list_slope_loading_page_kernel(
                 nc.vector.tensor_tensor(out=h[:, j], in0=acc[2][:], in1=h13[:, j], op=ALU.max)
             return h
 
-        def put_new(page, old, h):
-            nc.vector.tensor_tensor(out=page[:].indirect(idx2[:]), in0=old[:], in1=h[:], op=ALU.add)
+        def put_new(s):
+            nc.vector.tensor_tensor(out=page[s][:].indirect(idx2[:]), in0=old[s][:], in1=h[:], op=ALU.add)
 
-        def fetch_x(s, page, parts):
-            b, t = divmod(s, PACK)
-            width = NJ // parts
-            for u in range(parts):
-                j = slice(u * width, (u + 1) * width)
-                listed = idx3[:, u * width // 16 : (u + 1) * width // 16]
-                nc.vector.tensor_tensor(out=x[b][:, t, j], in0=page[:].indirect(listed), in1=asp[s][:, j], op=ALU.mult)
+        def fetch_x(s, j, into):
+            listed = idx3[:, j.start // 16 : j.stop // 16]
+            nc.vector.tensor_tensor(out=into, in0=page[s][:].indirect(listed), in1=asp[s][:, j], op=ALU.mult)
 
-        def round_x(b, u):
-            rounded = ring.tile([P, JH, PACK], BF16, name="x_bf", align_bytes=64)
+        def round_x(b, j):
+            rounded = ring.tile([P, j.stop - j.start, PACK], BF16, name="x_bf", align_bytes=64)
             nc.scalar.copy(
                 out=rounded[:].rearrange("p (c e) t -> p c t e", e=4),
-                in_=x[b][:, :, u * JH : (u + 1) * JH].rearrange("p t (c e) -> p c t e", e=4),
+                in_=x[b][:, :, j].rearrange("p t (c e) -> p c t e", e=4),
             )
             return rounded[:].rearrange("p j t -> p (j t)")
 
-        def mix_pass(bank, b, u, nb, pair):
-            for e in range(2):
-                t = 2 * pair + e
+        def round_last_block_early(j):
+            rounded = ring.tile([P, j.stop - j.start, PACK], BF16, name="x_bf", align_bytes=64)
+            nc.scalar.copy(
+                out=rounded[:, :, 0 : PACK - 1].rearrange("p (c e) t -> p c t e", e=4),
+                in_=x[1][:, 0 : PACK - 1, j].rearrange("p t (c e) -> p c t e", e=4),
+            )
+            return rounded
+
+        def mix_pass(bank, b, nb, ts, x_codes, x_scales):
+            w4_c, w4_s = w4_mx[b, nb]
+            for e, t in enumerate(ts):
                 own = slice(t * P, (t + 1) * P)
                 nc.tensor.matmul_mx(
                     out=bank[:, e, :],
-                    lhsT=w4_c[BLOCKS * b + nb][:, own].bitcast(FP8X4),
-                    lhsT_scale=w4_s[BLOCKS * b + nb][:, own],
-                    rhs=x_c[b][u][:].bitcast(FP8X4),
-                    rhs_scale=x_s[b][u][:],
-                    start=(b == 0 and e == 0),
-                    stop=(b == BLOCKS - 1 and e == 1),
+                    lhsT=w4_c[:, own].bitcast(FP8X4),
+                    lhsT_scale=w4_s[:, own],
+                    rhs=x_codes.bitcast(FP8X4),
+                    rhs_scale=x_scales,
+                    start=(b == 0 and t == ts[0]),
+                    stop=(b == BLOCKS - 1 and t == ts[-1]),
                 )
 
         nc.vector.memset(tab_s[:].bitcast(I32), 0)
         nc.gpsimd.memset(ws_raw[:].bitcast(I32), 0)
         nc.sync.dma_start(idx2[:], offs2)
         page = {0: load_page(0)}
-        load_scale_rows(nc.scalar, tab_s, tab_scales, 0)
+        load_scale_rows(tab_s, tab_scales, 0)
         nc.sync.dma_start(idx[:], offs)
         nc.sync.dma_start(out=tab_w[:].bitcast(I32), in_=tab_words[0].rearrange("p t i -> p (t i)").bitcast(I32))
-        load_scale_rows(nc.scalar, ws_raw, w3_scales, 4)
-        load_scale_rows(nc.scalar, ws_raw, w2_scales, 0)
+        load_scale_rows(ws_raw, w3_scales, 4)
+        load_scale_rows(ws_raw, w2_scales, 0)
         w1_raw = load_weight(w1_rows[:, :, 0:KP])
         nc.sync.dma_start(out=w3_raw[:], in_=w3_words[0].rearrange("p c i -> p (c i)").bitcast(I32))
         nc.sync.dma_start(out=w2_raw[:].bitcast(I32), in_=w2_words[0].bitcast(I32))
         page[1] = load_page(1)
         nc.sync.dma_start(idx3[:], offs3)
-        nc.sync.dma_start(out=asp[0][:], in_=aspect_rows[0, 0])
+        asp = {0: load_aspect(0)}
 
-        old = fetch_old(page[0])
-        rounded = round_weight(w1_raw)
+        old = {0: fetch_old(0)}
+        w1_bf = round_weight(w1_raw)
         nc.vector.tensor_copy(out=v_s[:], in_=tab_s[:].indirect(idx[:]))
         nc.vector.tensor_copy(
             out=w3_c[:].rearrange("p (b t m) -> p b m t", t=PACK, m=P),
@@ -185,7 +193,7 @@ def tile_list_slope_loading_page_kernel(
             out=w23_s[:].rearrange("p (b t m) -> p b t m", t=PACK, m=P),
             in_=ws_raw[:].rearrange("p (b m t) -> p b t m", t=PACK, m=P),
         )
-        quantize(w1_c[0], w1_s[0], rounded)
+        w1_mx = {0: quantize(w1_bf, "w1a")}
         for u in range(S // BANK):
             nc.vector.tensor_copy(
                 out=v_w[:, u * BANK : (u + 1) * BANK],
@@ -193,41 +201,55 @@ def tile_list_slope_loading_page_kernel(
             )
         h = features(0)
 
-        later_weights = [(w1_rows[:, :, KP:H], w1_c[1], w1_s[1])] + [
-            (w4_rows[b, :, :, nb * KP : (nb + 1) * KP], w4_c[BLOCKS * b + nb], w4_s[BLOCKS * b + nb])
-            for b in range(BLOCKS)
-            for nb in range(BLOCKS)
-        ]
+        w4_mx = {}
+        w4_bf = {}
         for s in range(SLICES):
             if s + 2 < SLICES:
                 page[s + 2] = load_page(s + 2)
             if s + 1 < SLICES:
-                nc.sync.dma_start(out=asp[s + 1][:], in_=aspect_rows[(s + 1) // PACK, (s + 1) % PACK])
-            if s < len(later_weights):
-                rows, codes, scales = later_weights[s]
-                rounded = round_weight(load_weight(rows))
-            put_new(page[s], old, h)
-            if s < len(later_weights):
-                quantize(codes, scales, rounded)
+                asp[s + 1] = load_aspect(s + 1)
+            if s == 0:
+                w1_bf = round_weight(load_weight(w1_rows[:, :, KP:H]))
+            if 1 <= s <= BLOCKS * BLOCKS:
+                b, nb = divmod(s - 1, BLOCKS)
+                w4_bf[b, nb] = round_weight(load_weight(w4_rows[b, :, :, nb * KP : (nb + 1) * KP]))
+            put_new(s)
+            if s == 0:
+                w1_mx[1] = quantize(w1_bf, "w1b")
+            if 1 <= s <= BLOCKS:
+                w4_mx[0, s - 1] = quantize(w4_bf[0, s - 1], "w4_%d" % (s - 1))
             if s == PACK:
-                for u in range(2):
-                    quantize(x_c[0][u], x_s[0][u], round_x(0, u))
+                x0_mx = [quantize(round_x(0, j), "x0_%d" % u) for u, j in enumerate(PIECES)]
             if s + 1 < SLICES:
-                old = fetch_old(page[s + 1])
+                old[s + 1] = fetch_old(s + 1)
                 h = features(s + 1)
-                fetch_x(s, page[s], 1)
+                fetch_x(s, slice(0, NJ), x[s // PACK][:, s % PACK, :])
 
-        parts = [(u, nb, pair) for u in range(2) for nb in range(BLOCKS) for pair in range(2)]
-        banks = [psum.tile([P, 2, JH], F32, name="bank%d" % i) for i in range(len(parts))]
-        for bank, part in zip(banks, parts):
-            mix_pass(bank, 0, *part)
-        fetch_x(SLICES - 1, page[SLICES - 1], 2)
-        for u in range(2):
-            quantize(x_c[1][u], x_s[1][u], round_x(1, u))
-        for bank, (u, nb, pair) in zip(banks, parts):
-            mix_pass(bank, 1, u, nb, pair)
-            j = slice(u * JH, (u + 1) * JH)
-            t = slice(2 * pair, 2 * pair + 2)
-            result = ring.tile([P, 2, JH], F32, name="result", bufs=8)
-            nc.vector.tensor_tensor(out=result[:], in0=bank[:], in1=x[nb][:, t, j], op=ALU.max)
-            nc.sync.dma_start(out=out_rows[nb, :, t, j], in_=result[:])
+        parts = []
+        for u, j in enumerate(PIECES):
+            per_bank = BANK // (j.stop - j.start)
+            for nb in range(BLOCKS):
+                for t0 in range(0, PACK, per_bank):
+                    bank = psum.tile([P, per_bank, j.stop - j.start], F32, name="bank%d" % len(parts))
+                    ts = range(t0, t0 + per_bank)
+                    mix_pass(bank, 0, nb, ts, x0_mx[u][0][:], x0_mx[u][1][:])
+                    parts.append((bank, u, nb, ts))
+        x1_bf = [round_last_block_early(j) for j in PIECES]
+        w4_mx[1, 0] = quantize(w4_bf[1, 0], "aspect%d" % (SLICES - 2))
+        for j, rounded, last in zip(PIECES, x1_bf, x_last):
+            fetch_x(SLICES - 1, j, last[:])
+            nc.scalar.copy(out=rounded[:, :, PACK - 1], in_=last[:])
+        x1_bf = [rounded[:].rearrange("p j t -> p (j t)") for rounded in x1_bf]
+        w4_mx[1, 1] = quantize(w4_bf[1, 1], "aspect%d" % (SLICES - 1))
+        x1_mx = [quantize(rounded, "x1_%d" % u) for u, rounded in enumerate(x1_bf)]
+        for bank, u, nb, ts in parts:
+            mix_pass(bank, 1, nb, ts, x1_mx[u][0][:], x1_mx[u][1][:])
+            j = PIECES[u]
+            result = ring.tile([P, len(ts), j.stop - j.start], F32, name="result", bufs=8)
+            held = min(ts.stop, PACK - nb) - ts.start
+            nc.vector.tensor_tensor(
+                out=result[:, 0:held, :], in0=bank[:, 0:held, :], in1=x[nb][:, ts.start : ts.start + held, j], op=ALU.max
+            )
+            if held < len(ts):
+                nc.vector.tensor_tensor(out=result[:, held, :], in0=bank[:, held, :], in1=x_last[u][:], op=ALU.max)
+            nc.sync.dma_start(out=out_rows[nb, :, ts.start : ts.stop, j], in_=result[:])

from contextlib import ExitStack

import concourse.mybir as mybir

K, H, T, S, T2, NJ = 512, 1024, 4096, 1024, 2048, 512
FLOPS = 2 * K * H * S * 3 + 2 * H * H * NJ

F32 = mybir.dt.float32
BF16 = mybir.dt.bfloat16
I32 = mybir.dt.int32
U32 = mybir.dt.uint32
U16 = mybir.dt.uint16
U8 = mybir.dt.uint8
FP8X4 = mybir.dt.float8_e4m3fn_x4
FP4X4 = mybir.dt.float4_e2m1fn_x4
ALU = mybir.AluOpType

P = 128
PACK = 4
KP = P * PACK
BANK = 512
BLOCKS = H // KP
SLICES = H // P
PIECES = (slice(0, NJ // 2), slice(NJ // 2, NJ))


def tile_list_slope_loading_page_kernel(
    tc, tab_words, tab_scales, offs, w1, w2_words, w2_scales, w3_words, w3_scales,
    page0, offs2, offs3, aspect, w4, out,
):
    nc = tc.nc
    page_rows = page0.rearrange("(b p t) c -> b t p c", p=P, t=PACK)
    aspect_rows = aspect.rearrange("(b p t) c -> b t p c", p=P, t=PACK)
    out_rows = out.rearrange("(b p t) c -> b p t c", p=P, t=PACK)
    w1_rows = w1.rearrange("(p i) c -> p i c", i=PACK)
    w4_rows = w4.rearrange("(b p i) c -> b p i c", p=P, i=PACK)

    with ExitStack() as ctx:
        keep = ctx.enter_context(tc.tile_pool(name="keep", bufs=1))
        ring = ctx.enter_context(tc.tile_pool(name="ring", bufs=2))
        pages = ctx.enter_context(tc.tile_pool(name="pages", bufs=4))
        psum = ctx.enter_context(tc.psum_pool(name="psum", bufs=1))

        idx = keep.tile([P, S // 16], U16, name="idx")
        idx2 = keep.tile([P, S // 16], U16, name="idx2")
        idx3 = keep.tile([P, NJ // 16], U16, name="idx3")
        tab_w = keep.tile([P, T], U32, name="tab_w")
        tab_s = keep.tile([P, T], U8, name="tab_s")
        v_w = keep.tile([P, S], U32, name="v_w", align_bytes=64)
        v_s = keep.tile([P, S], U8, name="v_s", align_bytes=64)
        w2_raw = keep.tile([P, 2 * H], U8, name="w2_raw")
        w3_raw = keep.tile([P, H], I32, name="w3_raw")
        ws_raw = keep.tile([P, H], U8, name="ws_raw")
        w2_c = keep.tile([P, 2 * H], U8, name="w2_c", align_bytes=64)
        w3_c = keep.tile([P, H], I32, name="w3_c", align_bytes=64)
        w23_s = keep.tile([P, H], U8, name="w23_s", align_bytes=64)
        x = [keep.tile([P, PACK - b, NJ], F32, name="x%d" % b) for b in range(BLOCKS)]
        x_last = [keep.tile([P, j.stop - j.start], F32, name="x_last%d" % u) for u, j in enumerate(PIECES)]

        def load_scale_rows(plane, rows, first):
            for q in range(4):
                nc.scalar.dma_start(
                    out=plane[32 * q + first : 32 * q + first + 4, :].bitcast(I32),
                    in_=rows[0, 4 * q : 4 * q + 4, :].bitcast(I32),
                )

        def load_page(s):
            page = pages.tile([P, T2], F32, name="page")
            nc.sync.dma_start(out=page[:], in_=page_rows[s // PACK, s % PACK])
            return page

        def load_aspect(s):
            rows = keep.tile([P, NJ], F32, name="aspect%d" % s, align_bytes=64)
            nc.sync.dma_start(out=rows[:], in_=aspect_rows[s // PACK, s % PACK])
            return rows

        def load_weight(rows):
            raw = ring.tile([P, PACK, KP], F32, name="w_raw", bufs=3)
            nc.sync.dma_start(out=raw[:], in_=rows)
            return raw

        def round_weight(raw):
            rounded = ring.tile([P, PACK * KP], BF16, name="w_bf", align_bytes=64)
            nc.scalar.copy(
                out=rounded[:].rearrange("p (t m i) -> p m t i", t=PACK, i=PACK),
                in_=raw[:].rearrange("p i (m t) -> p m t i", t=PACK),
            )
            return rounded[:]

        def quantize(rounded, tag):
            width = rounded.shape[1] // PACK
            codes = keep.tile([P, width], U32, name="codes", tag=tag, align_bytes=64)
            scales = keep.tile([P, width], U8, name="scales", tag=tag + "_scales", align_bytes=64)
            nc.vector.quantize_mx(out=codes[:].bitcast(FP8X4), scales=scales[:], in_=rounded)
            return codes, scales

        def fetch_old(s):
            old = ring.tile([P, S], F32, name="old")
            nc.vector.tensor_copy(out=old[:], in_=page[s][:].indirect(idx2[:]))
            return old

        def features(s):
            b, t = divmod(s, PACK)
            own = slice(t * P, (t + 1) * P)
            cols = slice(s * P, (s + 1) * P)
            w1_c, w1_s = w1_mx[b]
            h1 = ring.tile([P, S], F32, name="h1")
            h13 = ring.tile([P, S], F32, name="h13")
            h = ring.tile([P, S], F32, name="h")
            banks = []
            for u in range(S // BANK):
                j = slice(u * BANK, (u + 1) * BANK)
                rhs = dict(rhs=v_w[:, j].bitcast(FP8X4), rhs_scale=v_s[:, j], start=True, stop=True)
                acc = [psum.tile([P, BANK], F32, name="bank%d" % (3 * u + i)) for i in range(3)]
                nc.tensor.matmul_mx(out=acc[0][:], lhsT=w1_c[:, own].bitcast(FP8X4), lhsT_scale=w1_s[:, own], **rhs)
                nc.tensor.matmul_mx(out=acc[1][:], lhsT=w3_c[:, cols].bitcast(FP8X4), lhsT_scale=w23_s[4:P, cols], **rhs)
                nc.tensor.matmul_mx(
                    out=acc[2][:], lhsT=w2_c[:, 2 * s * P : 2 * (s + 1) * P].bitcast(FP4X4), lhsT_scale=w23_s[:, cols], **rhs
                )
                nc.scalar.copy(out=h1[:, j], in_=acc[0][:])
                banks.append((j, acc))
            for j, acc in banks:
                nc.vector.tensor_tensor(out=h13[:, j], in0=acc[1][:], in1=h1[:, j], op=ALU.max)
            for j, acc in banks:
                nc.vector.tensor_tensor(out=h[:, j], in0=acc[2][:], in1=h13[:, j], op=ALU.max)
            return h

        def put_new(s):
            nc.vector.tensor_tensor(out=page[s][:].indirect(idx2[:]), in0=old[s][:], in1=h[:], op=ALU.add)

        def fetch_x(s, j, into):
            listed = idx3[:, j.start // 16 : j.stop // 16]
            nc.vector.tensor_tensor(out=into, in0=page[s][:].indirect(listed), in1=asp[s][:, j], op=ALU.mult)

        def round_x(b, j):
            rounded = ring.tile([P, j.stop - j.start, PACK], BF16, name="x_bf", align_bytes=64)
            nc.scalar.copy(
                out=rounded[:].rearrange("p (c e) t -> p c t e", e=4),
                in_=x[b][:, :, j].rearrange("p t (c e) -> p c t e", e=4),
            )
            return rounded[:].rearrange("p j t -> p (j t)")

        def round_last_block_early(j):
            rounded = ring.tile([P, j.stop - j.start, PACK], BF16, name="x_bf", align_bytes=64)
            nc.scalar.copy(
                out=rounded[:, :, 0 : PACK - 1].rearrange("p (c e) t -> p c t e", e=4),
                in_=x[1][:, 0 : PACK - 1, j].rearrange("p t (c e) -> p c t e", e=4),
            )
            return rounded

        def mix_pass(bank, b, nb, ts, x_codes, x_scales):
            w4_c, w4_s = w4_mx[b, nb]
            for e, t in enumerate(ts):
                own = slice(t * P, (t + 1) * P)
                nc.tensor.matmul_mx(
                    out=bank[:, e, :],
                    lhsT=w4_c[:, own].bitcast(FP8X4),
                    lhsT_scale=w4_s[:, own],
                    rhs=x_codes.bitcast(FP8X4),
                    rhs_scale=x_scales,
                    start=(b == 0 and t == ts[0]),
                    stop=(b == BLOCKS - 1 and t == ts[-1]),
                )

        nc.vector.memset(tab_s[:].bitcast(I32), 0)
        nc.gpsimd.memset(ws_raw[:].bitcast(I32), 0)
        nc.sync.dma_start(idx2[:], offs2)
        page = {0: load_page(0)}
        load_scale_rows(tab_s, tab_scales, 0)
        nc.sync.dma_start(idx[:], offs)
        nc.sync.dma_start(out=tab_w[:].bitcast(I32), in_=tab_words[0].rearrange("p t i -> p (t i)").bitcast(I32))
        load_scale_rows(ws_raw, w3_scales, 4)
        load_scale_rows(ws_raw, w2_scales, 0)
        w1_raw = load_weight(w1_rows[:, :, 0:KP])
        nc.sync.dma_start(out=w3_raw[:], in_=w3_words[0].rearrange("p c i -> p (c i)").bitcast(I32))
        nc.sync.dma_start(out=w2_raw[:].bitcast(I32), in_=w2_words[0].bitcast(I32))
        page[1] = load_page(1)
        nc.sync.dma_start(idx3[:], offs3)
        asp = {0: load_aspect(0)}

        old = {0: fetch_old(0)}
        w1_bf = round_weight(w1_raw)
        nc.vector.tensor_copy(out=v_s[:], in_=tab_s[:].indirect(idx[:]))
        nc.vector.tensor_copy(
            out=w3_c[:].rearrange("p (b t m) -> p b m t", t=PACK, m=P),
            in_=w3_raw[:].rearrange("p (b m t) -> p b m t", t=PACK, m=P),
        )
        nc.vector.tensor_copy(
            out=w2_c[:].bitcast(U16).rearrange("p (b t m) -> p b t m", t=PACK, m=P),
            in_=w2_raw[:].bitcast(U16).rearrange("p (b m t) -> p b t m", t=PACK, m=P),
        )
        nc.vector.tensor_copy(
            out=w23_s[:].rearrange("p (b t m) -> p b t m", t=PACK, m=P),
            in_=ws_raw[:].rearrange("p (b m t) -> p b t m", t=PACK, m=P),
        )
        w1_mx = {0: quantize(w1_bf, "w1a")}
        for u in range(S // BANK):
            nc.vector.tensor_copy(
                out=v_w[:, u * BANK : (u + 1) * BANK],
                in_=tab_w[:].indirect(idx[:, u * BANK // 16 : (u + 1) * BANK // 16]),
            )
        h = features(0)

        w4_mx = {}
        w4_bf = {}
        for s in range(SLICES):
            if s + 2 < SLICES:
                page[s + 2] = load_page(s + 2)
            if s + 1 < SLICES:
                asp[s + 1] = load_aspect(s + 1)
            if s == 0:
                w1_bf = round_weight(load_weight(w1_rows[:, :, KP:H]))
            if 1 <= s <= BLOCKS * BLOCKS:
                b, nb = divmod(s - 1, BLOCKS)
                w4_bf[b, nb] = round_weight(load_weight(w4_rows[b, :, :, nb * KP : (nb + 1) * KP]))
            put_new(s)
            if s == 0:
                w1_mx[1] = quantize(w1_bf, "w1b")
            if 1 <= s <= BLOCKS:
                w4_mx[0, s - 1] = quantize(w4_bf[0, s - 1], "w4_%d" % (s - 1))
            if s == PACK:
                x0_mx = [quantize(round_x(0, j), "x0_%d" % u) for u, j in enumerate(PIECES)]
            if s + 1 < SLICES:
                old[s + 1] = fetch_old(s + 1)
                h = features(s + 1)
                fetch_x(s, slice(0, NJ), x[s // PACK][:, s % PACK, :])

        parts = []
        for u, j in enumerate(PIECES):
            per_bank = BANK // (j.stop - j.start)
            for nb in range(BLOCKS):
                for t0 in range(0, PACK, per_bank):
                    bank = psum.tile([P, per_bank, j.stop - j.start], F32, name="bank%d" % len(parts))
                    ts = range(t0, t0 + per_bank)
                    mix_pass(bank, 0, nb, ts, x0_mx[u][0][:], x0_mx[u][1][:])
                    parts.append((bank, u, nb, ts))
        x1_bf = [round_last_block_early(j) for j in PIECES]
        w4_mx[1, 0] = quantize(w4_bf[1, 0], "aspect%d" % (SLICES - 2))
        for j, rounded, last in zip(PIECES, x1_bf, x_last):
            fetch_x(SLICES - 1, j, last[:])
            nc.scalar.copy(out=rounded[:, :, PACK - 1], in_=last[:])
        x1_bf = [rounded[:].rearrange("p j t -> p (j t)") for rounded in x1_bf]
        w4_mx[1, 1] = quantize(w4_bf[1, 1], "aspect%d" % (SLICES - 1))
        x1_mx = [quantize(rounded, "x1_%d" % u) for u, rounded in enumerate(x1_bf)]
        for bank, u, nb, ts in parts:
            mix_pass(bank, 1, nb, ts, x1_mx[u][0][:], x1_mx[u][1][:])
            j = PIECES[u]
            result = ring.tile([P, len(ts), j.stop - j.start], F32, name="result", bufs=8)
            held = min(ts.stop, PACK - nb) - ts.start
            nc.vector.tensor_tensor(
                out=result[:, 0:held, :], in0=bank[:, 0:held, :], in1=x[nb][:, ts.start : ts.start + held, j], op=ALU.max
            )
            if held < len(ts):
                nc.vector.tensor_tensor(out=result[:, held, :], in0=bank[:, held, :], in1=x_last[u][:], op=ALU.max)
            nc.sync.dma_start(out=out_rows[nb, :, ts.start : ts.stop, j], in_=result[:])
